import numpy as np
import ml_dtypes

BF16 = ml_dtypes.bfloat16


def bf(x):
    return np.asarray(x, np.float32).astype(BF16)


def f32(x):
    return np.asarray(x, np.float32)


def f64(x):
    return np.asarray(x).astype(np.float64)


def striped(idx):
    return np.concatenate([l.reshape(-1, 16).T for l in idx])


def rows(idx, k):
    return np.tile(np.repeat(idx, 16, axis=0), (k // (16 * 8), 1))


def look(tab, idx):
    return np.take_along_axis(f64(tab), rows(idx, len(tab)), axis=1)


K, S, H, V, N = 128, 2048, 256, 1536, 1536


def setup_inputs():
    return {"z": bf(np.random.standard_normal((H, S))), "wt": bf(np.random.standard_normal((H, K)) / np.sqrt(H)), "y": f32(1.0 * np.random.standard_normal((K, V))), "offs": striped(np.stack([np.random.permutation(S)[:N] for _ in range(8)]))}


def reference(z, wt, y, offs):
    idx = np.stack([g.T.reshape(-1) for g in np.split(offs, 8)])
    tab = f64(wt).T @ f64(z)
    x = f64(y) / (1.0 + np.exp(-look(tab, idx)))
    return x

@@ -1,0 +1,51 @@
+import concourse.mybir as mybir
+
+BF16, F32, U16 = mybir.dt.bfloat16, mybir.dt.float32, mybir.dt.uint16
+SIGMOID = mybir.ActivationFunctionType.Sigmoid
+MULT = mybir.AluOpType.mult
+
+P = 128
+S = 2048
+N = 1536
+HALVES = 2
+BANK = 512
+PIECE = 512
+
+FLOPS = 2 * HALVES * 128 * P * S
+
+
+def tile_lookup_pjsig_out_kernel(tc, z, wt, y, offs, out):
+    nc = tc.nc
+    with (
+        tc.tile_pool(name="held", bufs=1) as held,
+        tc.tile_pool(name="ring", bufs=2) as ring,
+        tc.psum_pool(name="psum", bufs=4) as psum,
+    ):
+        weights = held.tile([P, HALVES, P], BF16, name="weights")
+        nc.sync.dma_start(weights[:], wt.rearrange("(p h) r -> p h r", h=HALVES))
+        z_rows = z.rearrange("(p h) i -> p h i", h=HALVES)
+        features = []
+        for c in range(S // BANK):
+            block = held.tile([P, HALVES, BANK], BF16, name=f"features{c}")
+            nc.sync.dma_start(block[:], z_rows[:, :, c * BANK : (c + 1) * BANK])
+            features.append(block)
+        offsets = held.tile([P, N // 16], U16, name="offsets")
+        nc.sync.dma_start(offsets[:], offs)
+        stream = held.tile([P, N], F32, name="stream")
+        nc.sync.dma_start(stream[:], y)
+
+        table = held.tile([P, S], F32, name="table")
+        for c in range(S // BANK):
+            scores = psum.tile([P, BANK], F32, name="scores")
+            for h in range(HALVES):
+                nc.tensor.matmul(
+                    scores[:], weights[:, h, :], features[c][:, h, :], start=h == 0, stop=h == HALVES - 1
+                )
+            nc.vector.tensor_copy(table[:, c * BANK : (c + 1) * BANK], scores[:])
+
+        for a in range(0, N, PIECE):
+            gate = ring.tile([P, PIECE], F32, name="gate")
+            nc.scalar.activation(gate[:], table[:].indirect(offsets[:, a // 16 : (a + PIECE) // 16]), SIGMOID)
+            gated = ring.tile([P, PIECE], F32, name="gated")
+            nc.vector.tensor_tensor(gated[:], gate[:], stream[:, a : a + PIECE], MULT)
+            nc.sync.dma_start(out[:, a : a + PIECE], gated[:])

@@ -9,6 +9,7 @@ S = 2048
 N = 1536
 HALVES = 2
 BANK = 512
+WARM_UPS = 5
 PIECE = 512
 
 FLOPS = 2 * HALVES * 128 * P * S
@@ -20,6 +21,7 @@ def tile_lookup_pjsig_out_kernel(tc, z, wt, y, offs, out):
         tc.tile_pool(name="held", bufs=1) as held,
         tc.tile_pool(name="ring", bufs=2) as ring,
         tc.psum_pool(name="psum", bufs=4) as psum,
+        tc.psum_pool(name="scrap", bufs=1) as scrap,
     ):
         weights = held.tile([P, HALVES, P], BF16, name="weights")
         nc.sync.dma_start(weights[:], wt.rearrange("(p h) r -> p h r", h=HALVES))
@@ -33,6 +35,12 @@ def tile_lookup_pjsig_out_kernel(tc, z, wt, y, offs, out):
         nc.sync.dma_start(offsets[:], offs)
         stream = held.tile([P, N], F32, name="stream")
         nc.sync.dma_start(stream[:], y)
+
+        zeros = held.tile([P, BANK], BF16, name="zeros")
+        nc.vector.memset(zeros[:], 0.0)
+        idle = scrap.tile([P, BANK], F32, name="idle")
+        for w in range(WARM_UPS):
+            nc.tensor.matmul(idle[:], zeros[:, :P], zeros[:], start=True, stop=True)
 
         table = held.tile([P, S], F32, name="table")
         for c in range(S // BANK):

@@ -1,6 +1,7 @@
 import concourse.mybir as mybir
 
 BF16, F32, U16 = mybir.dt.bfloat16, mybir.dt.float32, mybir.dt.uint16
+COPY = mybir.ActivationFunctionType.Copy
 SIGMOID = mybir.ActivationFunctionType.Sigmoid
 MULT = mybir.AluOpType.mult
 
@@ -8,9 +9,11 @@ P = 128
 S = 2048
 N = 1536
 HALVES = 2
-BANK = 512
-WARM_UPS = 5
+LOAD = 512
+SCORES = 256
 PIECE = 512
+WARM_UPS = 3
+WARM_COLS = 512
 
 FLOPS = 2 * HALVES * 128 * P * S
 
@@ -20,40 +23,49 @@ def tile_lookup_pjsig_out_kernel(tc, z, wt, y, offs, out):
     with (
         tc.tile_pool(name="held", bufs=1) as held,
         tc.tile_pool(name="ring", bufs=2) as ring,
-        tc.psum_pool(name="psum", bufs=4) as psum,
+        tc.psum_pool(name="psum", bufs=6) as psum,
         tc.psum_pool(name="scrap", bufs=1) as scrap,
     ):
         weights = held.tile([P, HALVES, P], BF16, name="weights")
-        nc.sync.dma_start(weights[:], wt.rearrange("(p h) r -> p h r", h=HALVES))
+        nc.scalar.dma_start(weights[:], wt.rearrange("(p h) r -> p h r", h=HALVES))
+        offsets = held.tile([P, N // 16], U16, name="offsets")
         z_rows = z.rearrange("(p h) i -> p h i", h=HALVES)
         features = []
-        for c in range(S // BANK):
-            block = held.tile([P, HALVES, BANK], BF16, name=f"features{c}")
-            nc.sync.dma_start(block[:], z_rows[:, :, c * BANK : (c + 1) * BANK])
+        for c in range(S // LOAD):
+            block = held.tile([P, HALVES, LOAD], BF16, name=f"features{c}")
+            nc.sync.dma_start(block[:], z_rows[:, :, c * LOAD : (c + 1) * LOAD])
             features.append(block)
-        offsets = held.tile([P, N // 16], U16, name="offsets")
         nc.sync.dma_start(offsets[:], offs)
         stream = held.tile([P, N], F32, name="stream")
         nc.sync.dma_start(stream[:], y)
 
-        zeros = held.tile([P, BANK], BF16, name="zeros")
+        zeros = held.tile([P, WARM_COLS], BF16, name="zeros")
         nc.vector.memset(zeros[:], 0.0)
-        idle = scrap.tile([P, BANK], F32, name="idle")
+        half = held.tile([P, 1], F32, name="half")
+        nc.scalar.activation(half[:], zeros[:, :1], SIGMOID)
+        idle = scrap.tile([P, WARM_COLS], F32, name="idle")
         for w in range(WARM_UPS):
             nc.tensor.matmul(idle[:], zeros[:, :P], zeros[:], start=True, stop=True)
 
         table = held.tile([P, S], F32, name="table")
-        for c in range(S // BANK):
-            scores = psum.tile([P, BANK], F32, name="scores")
+        for c in range(S // SCORES):
+            block, b = features[c * SCORES // LOAD], c * SCORES % LOAD
+            scores = psum.tile([P, SCORES], F32, name="scores")
             for h in range(HALVES):
                 nc.tensor.matmul(
-                    scores[:], weights[:, h, :], features[c][:, h, :], start=h == 0, stop=h == HALVES - 1
+                    scores[:], weights[:, h, :], block[:, h, b : b + SCORES], start=h == 0, stop=h == HALVES - 1
                 )
-            nc.vector.tensor_copy(table[:, c * BANK : (c + 1) * BANK], scores[:])
+            columns = table[:, c * SCORES : (c + 1) * SCORES]
+            if c % 2 == 0:
+                nc.scalar.activation(columns, scores[:], COPY)
+            else:
+                nc.vector.tensor_copy(columns, scores[:])
 
         for a in range(0, N, PIECE):
             gate = ring.tile([P, PIECE], F32, name="gate")
             nc.scalar.activation(gate[:], table[:].indirect(offsets[:, a // 16 : (a + PIECE) // 16]), SIGMOID)
             gated = ring.tile([P, PIECE], F32, name="gated")
-            nc.vector.tensor_tensor(gated[:], gate[:], stream[:, a : a + PIECE], MULT)
-            nc.sync.dma_start(out[:, a : a + PIECE], gated[:])
+            for b in range(0, PIECE, PIECE // 2):
+                part = slice(b, b + PIECE // 2)
+                nc.vector.tensor_tensor(gated[:, part], gate[:, part], stream[:, a + b : a + b + PIECE // 2], MULT)
+                nc.sync.dma_start(out[:, a + b : a + b + PIECE // 2], gated[:, part])

import concourse.mybir as mybir

BF16, F32, U16 = mybir.dt.bfloat16, mybir.dt.float32, mybir.dt.uint16
COPY = mybir.ActivationFunctionType.Copy
SIGMOID = mybir.ActivationFunctionType.Sigmoid
MULT = mybir.AluOpType.mult

P = 128
S = 2048
N = 1536
HALVES = 2
LOAD = 512
SCORES = 256
PIECE = 512
WARM_UPS = 3
WARM_COLS = 512

FLOPS = 2 * HALVES * 128 * P * S


def tile_lookup_pjsig_out_kernel(tc, z, wt, y, offs, out):
    nc = tc.nc
    with (
        tc.tile_pool(name="held", bufs=1) as held,
        tc.tile_pool(name="ring", bufs=2) as ring,
        tc.psum_pool(name="psum", bufs=6) as psum,
        tc.psum_pool(name="scrap", bufs=1) as scrap,
    ):
        weights = held.tile([P, HALVES, P], BF16, name="weights")
        nc.scalar.dma_start(weights[:], wt.rearrange("(p h) r -> p h r", h=HALVES))
        offsets = held.tile([P, N // 16], U16, name="offsets")
        z_rows = z.rearrange("(p h) i -> p h i", h=HALVES)
        features = []
        for c in range(S // LOAD):
            block = held.tile([P, HALVES, LOAD], BF16, name=f"features{c}")
            nc.sync.dma_start(block[:], z_rows[:, :, c * LOAD : (c + 1) * LOAD])
            features.append(block)
        nc.sync.dma_start(offsets[:], offs)
        stream = held.tile([P, N], F32, name="stream")
        nc.sync.dma_start(stream[:], y)

        zeros = held.tile([P, WARM_COLS], BF16, name="zeros")
        nc.vector.memset(zeros[:], 0.0)
        half = held.tile([P, 1], F32, name="half")
        nc.scalar.activation(half[:], zeros[:, :1], SIGMOID)
        idle = scrap.tile([P, WARM_COLS], F32, name="idle")
        for w in range(WARM_UPS):
            nc.tensor.matmul(idle[:], zeros[:, :P], zeros[:], start=True, stop=True)

        table = held.tile([P, S], F32, name="table")
        for c in range(S // SCORES):
            block, b = features[c * SCORES // LOAD], c * SCORES % LOAD
            scores = psum.tile([P, SCORES], F32, name="scores")
            for h in range(HALVES):
                nc.tensor.matmul(
                    scores[:], weights[:, h, :], block[:, h, b : b + SCORES], start=h == 0, stop=h == HALVES - 1
                )
            columns = table[:, c * SCORES : (c + 1) * SCORES]
            if c % 2 == 0:
                nc.scalar.activation(columns, scores[:], COPY)
            else:
                nc.vector.tensor_copy(columns, scores[:])

        for a in range(0, N, PIECE):
            gate = ring.tile([P, PIECE], F32, name="gate")
            nc.scalar.activation(gate[:], table[:].indirect(offsets[:, a // 16 : (a + PIECE) // 16]), SIGMOID)
            gated = ring.tile([P, PIECE], F32, name="gated")
            for b in range(0, PIECE, PIECE // 2):
                part = slice(b, b + PIECE // 2)
                nc.vector.tensor_tensor(gated[:, part], gate[:, part], stream[:, a + b : a + b + PIECE // 2], MULT)
                nc.sync.dma_start(out[:, a + b : a + b + PIECE // 2], gated[:, part])
